import numpy as np
import ml_dtypes


def mxq(x, axis, fmt="e4m3"):
    dtype, down = {"e4m3": (ml_dtypes.float8_e4m3fn, 7), "e5m2": (ml_dtypes.float8_e5m2, 14)}[fmt]
    v = np.moveaxis(np.asarray(x, np.float32).astype(ml_dtypes.bfloat16).astype(np.float64), axis, -1)
    blocks = v.reshape(v.shape[:-1] + (-1, 32))
    amax = np.abs(blocks).max(-1, keepdims=True)
    byte = np.maximum(np.where(amax > 0, np.frexp(amax)[1] - 1 + 127, 0) - down, 1)
    scale = np.exp2(byte - 127.0)
    codes = (blocks / scale).astype(np.float32).astype(dtype).astype(np.float64)
    return np.moveaxis((codes * scale).reshape(v.shape), -1, axis)


WIDE = False


def mx_kscale(k):
    if not WIDE:
        return np.ones(k)
    levels = np.array([10, -10, 5, -5, 0])
    if k % 512:
        return np.exp2(np.random.permutation(np.resize(levels, k // 32))).repeat(32)
    a = np.empty((k // 512, 16))
    for p in range(k // 512):
        a[p, :8] = np.random.permutation(np.resize(levels, 8))
        for g in range(8):
            far = levels[np.abs(levels - a[p, g]) >= 10]
            a[p, g + 8] = far[np.random.randint(len(far))]
    return np.exp2(a.ravel()).repeat(32)


def f64(x):
    return np.asarray(x).astype(np.float64)


def striped(idx):
    return np.tile(np.asarray(idx).reshape(-1, 16).T, (8, 1)).astype(np.uint16)


def unstriped(offs):
    return offs[:16].T.reshape(-1).astype(np.int64)


E2M1 = np.array([0.0, 0.5, 1.0, 1.5, 2.0, 3.0, 4.0, 6.0, -0.0, -0.5, -1.0, -1.5, -2.0, -3.0, -4.0, -6.0])


def pack_weight(w, fmt):
    k, n = w.shape
    w = f64(np.asarray(w, np.float32).astype(ml_dtypes.bfloat16)).reshape(k // 32, 32, n)
    amax = np.abs(w).max(1)
    if fmt == "e4m3":
        byte = np.frexp(amax)[1] - 1 + 127 - 7
    else:
        mant, ex = np.frexp(amax / 6.0)
        byte = np.where(mant > 0.5, ex, ex - 1) + 127
    byte = np.clip(np.where(amax > 0, byte, 1), 1, 254)
    scaled = (w * np.exp2(127.0 - byte)[:, None, :]).reshape(k, n).astype(np.float32)
    by_word = np.ascontiguousarray(scaled.reshape(k // 512, 128, 4, n).transpose(0, 1, 3, 2))
    if fmt == "e4m3":
        words = by_word.astype(ml_dtypes.float8_e4m3fn).view(np.uint8)
    else:
        c = by_word.astype(ml_dtypes.float4_e2m1fn).view(np.uint8) & 0xF
        words = (c[..., 0::2] | (c[..., 1::2] << 4)).reshape(k // 512, 128, 2 * n)
    return np.ascontiguousarray(words), np.ascontiguousarray(byte.astype(np.uint8).reshape(k // 512, 16, n))


def unpack_weight(words, scales, fmt):
    g, _, n = scales.shape
    words = np.ascontiguousarray(words).reshape(g, 128, n, -1)
    if fmt == "e4m3":
        vals = words.view(ml_dtypes.float8_e4m3fn).astype(np.float64)
    else:
        nib = np.empty((g, 128, n, 4), np.uint8)
        nib[..., 0::2] = words & 0xF
        nib[..., 1::2] = words >> 4
        vals = E2M1[nib]
    vals = vals * np.repeat(np.exp2(scales.astype(np.float64) - 127.0), 8, axis=1)[..., None]
    return vals.transpose(0, 1, 3, 2).reshape(g * 512, n)


def sigmoid(v):
    return 1.0 / (1.0 + np.exp(-v))


K, R, F, T, J, U = 512, 128, 512, 2048, 512, 1024


def setup_inputs():
    n = np.random.standard_normal
    idx = np.random.permutation(T)[:J]
    idx2 = np.random.permutation(U)[:J]
    fk = mx_kscale(K)
    tabp = pack_weight(n((K, T)) / fk[:, None], "e4m3")
    dtabp = pack_weight(n((K, T)) / fk[:, None], "e4m3")
    return {
        "tab_words": tabp[0],
        "tab_scales": tabp[1],
        "dtab_words": dtabp[0],
        "dtab_scales": dtabp[1],
        "w1": (n((K, R)) * 1 / np.sqrt(K) * fk[:, None]).astype(np.float32),
        "w2": (n((K, R)) * 1.4 / np.sqrt(K) * fk[:, None]).astype(np.float32),
        "bias": (np.random.uniform(-0.5, 0.5, (R, 1))).astype(np.float32),
        "carry": (n((R, U)) * 0.7).astype(np.float32),
        "og": (np.random.uniform(0.5, 2.0, (R, 1))).astype(np.float32),
        "base": (0.3 * n((R, J))).astype(np.float32),
        "offs": striped(idx),
        "offs2": striped(idx2),
    }


def reference(tab_words, tab_scales, dtab_words, dtab_scales, w1, w2, bias, carry, og, base, offs, offs2):
    idx = unstriped(offs)
    idx2 = unstriped(offs2)
    tabu = unpack_weight(tab_words, tab_scales, "e4m3")
    dtabu = unpack_weight(dtab_words, dtab_scales, "e4m3")
    w1q = mxq(f64(w1), 0, "e4m3")
    tabidxg = tabu[:, idx]
    a = w1q.T @ tabidxg
    dtabidxg = dtabu[:, idx]
    ta = w1q.T @ dtabidxg
    w2q = mxq(f64(w2), 0, "e4m3")
    b = w2q.T @ tabidxg
    tb = w2q.T @ dtabidxg
    h1 = np.tanh(a)
    gt = sigmoid(b + f64(bias))
    th1 = ta * (1.0 - np.square(h1))
    tgt = tb * gt * (1.0 - gt)
    tu1 = th1 * gt + tgt * (h1 - f64(carry)[:, idx2])
    y = tu1 * f64(og) + f64(base)
    return y

@@ -1,0 +1,163 @@
+from contextlib import ExitStack
+
+import concourse.mybir as mybir
+
+K, R, T, J, U = 512, 128, 2048, 512, 1024
+FLOPS = 4 * 2 * K * R * J
+
+F32 = mybir.dt.float32
+BF16 = mybir.dt.bfloat16
+I32 = mybir.dt.int32
+U32 = mybir.dt.uint32
+U16 = mybir.dt.uint16
+U8 = mybir.dt.uint8
+FP8X4 = mybir.dt.float8_e4m3fn_x4
+ACT = mybir.ActivationFunctionType
+ALU = mybir.AluOpType
+
+P = 128
+PACK = 4
+HALVES = 2
+JH = J // HALVES
+LIST_ROWS = 16
+DTAB_PLANE = 4
+
+
+def tile_attend_tccarrymix_kernel(
+    tc, tab_words, tab_scales, dtab_words, dtab_scales, w1, w2, bias, carry, og, base, offs, offs2, out
+):
+    nc = tc.nc
+    with ExitStack() as ctx:
+        sb = ctx.enter_context(tc.tile_pool(name="sb", bufs=1))
+        ps = ctx.enter_context(tc.psum_pool(name="ps", bufs=1))
+
+        idx = sb.tile([P, J // LIST_ROWS], U16, name="idx")
+        idx2 = sb.tile([P, J // LIST_ROWS], U16, name="idx2")
+        tab_w = sb.tile([P, T], I32, name="tab_w", align_bytes=64)
+        dtab_w = sb.tile([P, T], I32, name="dtab_w", align_bytes=64)
+        tab_s = sb.tile([P, T], U8, name="tab_s", tag="slot_base", align_bytes=64)
+        dtab_s = sb.tile([P, T], U8, name="dtab_s", align_bytes=64)
+        w1_raw = sb.tile([P, PACK, R], F32, name="w1_raw")
+        w2_raw = sb.tile([P, PACK, R], F32, name="w2_raw")
+        carry_sb = sb.tile([P, U], F32, name="carry_sb")
+        bias_sb = sb.tile([P, 1], F32, name="bias_sb")
+        og_sb = sb.tile([P, 1], F32, name="og_sb")
+
+        def load_scales(queue, plane, src, first):
+            rows = src[0].bitcast(I32)
+            for q in range(4):
+                queue.dma_start(
+                    out=plane[32 * q + first : 32 * q + first + 4, :].bitcast(I32), in_=rows[4 * q : 4 * q + 4, :]
+                )
+
+        def load_words(dst, src):
+            nc.sync.dma_start(out=dst[:], in_=src[0].rearrange("p n t -> p (n t)").bitcast(I32))
+
+        warm_in = sb.tile([P, 1], F32, name="warm_in")
+        warm_out = sb.tile([P, 1], F32, name="warm_out")
+        nc.gpsimd.memset(warm_in[:], 0.0)
+        nc.scalar.activation(warm_out[:], warm_in[:], ACT.Sigmoid)
+        nc.vector.memset(tab_s[:].bitcast(I32), 0)
+        nc.gpsimd.dma_start(out=bias_sb[:], in_=bias)
+        nc.gpsimd.memset(dtab_s[:].bitcast(I32), 0)
+        nc.sync.dma_start(idx[:], offs)
+        nc.sync.dma_start(idx2[:], offs2)
+        nc.sync.dma_start(out=w1_raw[:], in_=w1.rearrange("(p j) r -> p j r", j=PACK))
+        load_scales(nc.sync, tab_s, tab_scales, 0)
+        load_words(tab_w, tab_words)
+        nc.sync.dma_start(out=w2_raw[:], in_=w2.rearrange("(p j) r -> p j r", j=PACK))
+        nc.sync.dma_start(out=carry_sb[:], in_=carry)
+        load_words(dtab_w, dtab_words)
+        load_scales(nc.scalar, dtab_s, dtab_scales, DTAB_PLANE)
+        nc.gpsimd.dma_start(out=og_sb[:], in_=og)
+
+        def quantise(raw, name):
+            grouped = sb.tile([P, R, PACK], BF16, name=name + "_g", align_bytes=64)
+            nc.scalar.copy(out=grouped[:], in_=raw[:].rearrange("p j r -> p r j"))
+            codes = sb.tile([P, R], U32, name=name + "_c", align_bytes=64)
+            scales = sb.tile([P, R], U8, name=name + "_s", align_bytes=64)
+            nc.vector.quantize_mx(
+                out=codes[:].bitcast(FP8X4), scales=scales[:], in_=grouped[:].rearrange("p r j -> p (r j)")
+            )
+            return codes, scales
+
+        def half_list(lst, h):
+            n = JH // LIST_ROWS
+            return lst[:, h * n : (h + 1) * n]
+
+        def cols(h):
+            return slice(h * JH, (h + 1) * JH)
+
+        def product(name, wq, words, plane, first, h):
+            acc = ps.tile([P, JH], F32, name=name)
+            nc.tensor.matmul_mx(
+                out=acc[:],
+                lhsT=wq[0][:].bitcast(FP8X4),
+                lhsT_scale=wq[1][:],
+                rhs=words[:].bitcast(FP8X4),
+                rhs_scale=plane[first:P, cols(h)],
+                start=True,
+                stop=True,
+            )
+            return acc
+
+        tab_sg = sb.tile([P, J], U8, name="tab_sg", align_bytes=64)
+        nc.vector.tensor_copy(tab_sg[:], tab_s[:].indirect(idx[:]))
+        w1q = quantise(w1_raw, "w1")
+        dtab_sg = sb.tile([P, J], U8, name="dtab_sg", align_bytes=64)
+        nc.vector.tensor_copy(dtab_sg[:], dtab_s[:].indirect(idx[:]))
+        w2q = quantise(w2_raw, "w2")
+
+        base_sb = sb.tile([P, J], F32, name="base_sb", tag="slot_base", align_bytes=64)
+        nc.sync.dma_start(out=base_sb[:], in_=base)
+
+        hs, gs, hsqs, gsqs = [], [], [], []
+        for h in range(HALVES):
+            tg = sb.tile([P, JH], U32, name="tab_g%d" % h, align_bytes=64)
+            nc.vector.tensor_copy(tg[:], tab_w[:].bitcast(U32).indirect(half_list(idx, h)))
+            a = product("a%d" % h, w1q, tg, tab_sg, 0, h)
+            b = product("b%d" % h, w2q, tg, tab_sg, 0, h)
+            h1 = sb.tile([P, JH], F32, name="h1_%d" % h)
+            gt = sb.tile([P, JH], F32, name="gt_%d" % h)
+            hsq = sb.tile([P, JH], F32, name="hsq_%d" % h)
+            gsq = sb.tile([P, JH], F32, name="gsq_%d" % h)
+            nc.scalar.activation(h1[:], a[:], ACT.Tanh)
+            nc.scalar.activation(gt[:], b[:], ACT.Sigmoid, bias=bias_sb[:])
+            nc.scalar.activation(hsq[:], h1[:], ACT.Square)
+            nc.scalar.activation(gsq[:], gt[:], ACT.Square, bias=-0.5)
+            hs.append(h1)
+            gs.append(gt)
+            hsqs.append(hsq)
+            gsqs.append(gsq)
+
+        carry_g = sb.tile([P, J], F32, name="carry_g")
+        nc.vector.tensor_copy(carry_g[:], carry_sb[:].indirect(idx2[:]))
+
+        fa, fb = [], []
+        for h in range(HALVES):
+            diff = sb.tile([P, JH], F32, name="diff%d" % h)
+            nc.vector.tensor_tensor(diff[:], carry_g[:, cols(h)], hs[h][:], ALU.subtract)
+            neg_a = sb.tile([P, JH], F32, name="neg_a%d" % h)
+            nc.vector.scalar_tensor_tensor(neg_a[:], hsqs[h][:], 1.0, gs[h][:], ALU.subtract, ALU.mult)
+            fac_b = sb.tile([P, JH], F32, name="fac_b%d" % h)
+            nc.vector.scalar_tensor_tensor(fac_b[:], gsqs[h][:], 0.25, diff[:], ALU.subtract, ALU.mult)
+            fa.append(neg_a)
+            fb.append(fac_b)
+
+        tas, tbs = [], []
+        for h in range(HALVES):
+            dg = sb.tile([P, JH], U32, name="dtab_g%d" % h, align_bytes=64)
+            nc.vector.tensor_copy(dg[:], dtab_w[:].bitcast(U32).indirect(half_list(idx, h)))
+            tas.append(product("ta%d" % h, w1q, dg, dtab_sg, DTAB_PLANE, h))
+            tbs.append(product("tb%d" % h, w2q, dg, dtab_sg, DTAB_PLANE, h))
+
+        m1 = [sb.tile([P, JH], F32, name="m1_%d" % h) for h in range(HALVES)]
+        m2 = [sb.tile([P, JH], F32, name="m2_%d" % h) for h in range(HALVES)]
+        s1 = [sb.tile([P, JH], F32, name="s1_%d" % h) for h in range(HALVES)]
+        y = [sb.tile([P, JH], F32, name="y_%d" % h) for h in range(HALVES)]
+        for h in range(HALVES):
+            nc.vector.scalar_tensor_tensor(m1[h][:], tas[h][:], og_sb[:], fa[h][:], ALU.mult, ALU.mult)
+            nc.vector.scalar_tensor_tensor(m2[h][:], tbs[h][:], og_sb[:], fb[h][:], ALU.mult, ALU.mult)
+            nc.vector.tensor_tensor(s1[h][:], base_sb[:, cols(h)], m1[h][:], ALU.subtract)
+            nc.vector.tensor_tensor(y[h][:], s1[h][:], m2[h][:], ALU.add)
+            nc.sync.dma_start(out=out[:, cols(h)], in_=y[h][:])

@@ -35,41 +35,43 @@ def tile_attend_tccarrymix_kernel(
         idx2 = sb.tile([P, J // LIST_ROWS], U16, name="idx2")
         tab_w = sb.tile([P, T], I32, name="tab_w", align_bytes=64)
         dtab_w = sb.tile([P, T], I32, name="dtab_w", align_bytes=64)
-        tab_s = sb.tile([P, T], U8, name="tab_s", tag="slot_base", align_bytes=64)
+        tab_s = sb.tile([P, T], U8, name="tab_s", align_bytes=64)
         dtab_s = sb.tile([P, T], U8, name="dtab_s", align_bytes=64)
         w1_raw = sb.tile([P, PACK, R], F32, name="w1_raw")
         w2_raw = sb.tile([P, PACK, R], F32, name="w2_raw")
         carry_sb = sb.tile([P, U], F32, name="carry_sb")
+        base_sb = sb.tile([P, J], F32, name="base_sb")
         bias_sb = sb.tile([P, 1], F32, name="bias_sb")
         og_sb = sb.tile([P, 1], F32, name="og_sb")
 
-        def load_scales(queue, plane, src, first):
+        def load_scales(plane, src, first):
             rows = src[0].bitcast(I32)
             for q in range(4):
-                queue.dma_start(
+                nc.sync.dma_start(
                     out=plane[32 * q + first : 32 * q + first + 4, :].bitcast(I32), in_=rows[4 * q : 4 * q + 4, :]
                 )
 
         def load_words(dst, src):
             nc.sync.dma_start(out=dst[:], in_=src[0].rearrange("p n t -> p (n t)").bitcast(I32))
 
-        warm_in = sb.tile([P, 1], F32, name="warm_in")
-        warm_out = sb.tile([P, 1], F32, name="warm_out")
-        nc.gpsimd.memset(warm_in[:], 0.0)
-        nc.scalar.activation(warm_out[:], warm_in[:], ACT.Sigmoid)
         nc.vector.memset(tab_s[:].bitcast(I32), 0)
-        nc.gpsimd.dma_start(out=bias_sb[:], in_=bias)
-        nc.gpsimd.memset(dtab_s[:].bitcast(I32), 0)
+        nc.vector.memset(dtab_s[:].bitcast(I32), 0)
         nc.sync.dma_start(idx[:], offs)
         nc.sync.dma_start(idx2[:], offs2)
         nc.sync.dma_start(out=w1_raw[:], in_=w1.rearrange("(p j) r -> p j r", j=PACK))
-        load_scales(nc.sync, tab_s, tab_scales, 0)
+        load_scales(tab_s, tab_scales, 0)
         load_words(tab_w, tab_words)
+        load_scales(dtab_s, dtab_scales, DTAB_PLANE)
         nc.sync.dma_start(out=w2_raw[:], in_=w2.rearrange("(p j) r -> p j r", j=PACK))
         nc.sync.dma_start(out=carry_sb[:], in_=carry)
         load_words(dtab_w, dtab_words)
-        load_scales(nc.scalar, dtab_s, dtab_scales, DTAB_PLANE)
+        nc.sync.dma_start(out=base_sb[:], in_=base)
+        nc.gpsimd.dma_start(out=bias_sb[:], in_=bias)
         nc.gpsimd.dma_start(out=og_sb[:], in_=og)
+        half_bias = sb.tile([P, 1], F32, name="half_bias")
+        half_og = sb.tile([P, 1], F32, name="half_og")
+        nc.gpsimd.tensor_scalar(half_bias[:], bias_sb[:], 0.5, None, ALU.mult)
+        nc.gpsimd.tensor_scalar(half_og[:], og_sb[:], 0.5, None, ALU.mult)
 
         def quantise(raw, name):
             grouped = sb.tile([P, R, PACK], BF16, name=name + "_g", align_bytes=64)
@@ -104,44 +106,36 @@ def tile_attend_tccarrymix_kernel(
         tab_sg = sb.tile([P, J], U8, name="tab_sg", align_bytes=64)
         nc.vector.tensor_copy(tab_sg[:], tab_s[:].indirect(idx[:]))
         w1q = quantise(w1_raw, "w1")
-        dtab_sg = sb.tile([P, J], U8, name="dtab_sg", align_bytes=64)
-        nc.vector.tensor_copy(dtab_sg[:], dtab_s[:].indirect(idx[:]))
         w2q = quantise(w2_raw, "w2")
 
-        base_sb = sb.tile([P, J], F32, name="base_sb", tag="slot_base", align_bytes=64)
-        nc.sync.dma_start(out=base_sb[:], in_=base)
-
-        hs, gs, hsqs, gsqs = [], [], [], []
+        hs, ts, hsqs = [], [], []
         for h in range(HALVES):
             tg = sb.tile([P, JH], U32, name="tab_g%d" % h, align_bytes=64)
             nc.vector.tensor_copy(tg[:], tab_w[:].bitcast(U32).indirect(half_list(idx, h)))
             a = product("a%d" % h, w1q, tg, tab_sg, 0, h)
             b = product("b%d" % h, w2q, tg, tab_sg, 0, h)
             h1 = sb.tile([P, JH], F32, name="h1_%d" % h)
-            gt = sb.tile([P, JH], F32, name="gt_%d" % h)
+            th = sb.tile([P, JH], F32, name="th_%d" % h)
             hsq = sb.tile([P, JH], F32, name="hsq_%d" % h)
-            gsq = sb.tile([P, JH], F32, name="gsq_%d" % h)
             nc.scalar.activation(h1[:], a[:], ACT.Tanh)
-            nc.scalar.activation(gt[:], b[:], ACT.Sigmoid, bias=bias_sb[:])
+            nc.scalar.activation(th[:], b[:], ACT.Tanh, bias=half_bias[:], scale=0.5)
             nc.scalar.activation(hsq[:], h1[:], ACT.Square)
-            nc.scalar.activation(gsq[:], gt[:], ACT.Square, bias=-0.5)
             hs.append(h1)
-            gs.append(gt)
+            ts.append(th)
             hsqs.append(hsq)
-            gsqs.append(gsq)
 
-        carry_g = sb.tile([P, J], F32, name="carry_g")
-        nc.vector.tensor_copy(carry_g[:], carry_sb[:].indirect(idx2[:]))
+        dtab_sg = sb.tile([P, J], U8, name="dtab_sg", align_bytes=64)
+        nc.vector.tensor_copy(dtab_sg[:], dtab_s[:].indirect(idx[:]))
 
-        fa, fb = [], []
+        diffs = []
         for h in range(HALVES):
             diff = sb.tile([P, JH], F32, name="diff%d" % h)
-            nc.vector.tensor_tensor(diff[:], carry_g[:, cols(h)], hs[h][:], ALU.subtract)
-            neg_a = sb.tile([P, JH], F32, name="neg_a%d" % h)
-            nc.vector.scalar_tensor_tensor(neg_a[:], hsqs[h][:], 1.0, gs[h][:], ALU.subtract, ALU.mult)
+            nc.vector.tensor_tensor(diff[:], carry_sb[:].indirect(half_list(idx2, h)), hs[h][:], ALU.subtract)
+            diffs.append(diff)
+        fb = []
+        for h in range(HALVES):
             fac_b = sb.tile([P, JH], F32, name="fac_b%d" % h)
-            nc.vector.scalar_tensor_tensor(fac_b[:], gsqs[h][:], 0.25, diff[:], ALU.subtract, ALU.mult)
-            fa.append(neg_a)
+            nc.vector.scalar_tensor_tensor(fac_b[:], ts[h][:], 1.0, diffs[h][:], ALU.subtract, ALU.mult)
             fb.append(fac_b)
 
         tas, tbs = [], []
@@ -151,13 +145,14 @@ def tile_attend_tccarrymix_kernel(
             tas.append(product("ta%d" % h, w1q, dg, dtab_sg, DTAB_PLANE, h))
             tbs.append(product("tb%d" % h, w2q, dg, dtab_sg, DTAB_PLANE, h))
 
-        m1 = [sb.tile([P, JH], F32, name="m1_%d" % h) for h in range(HALVES)]
-        m2 = [sb.tile([P, JH], F32, name="m2_%d" % h) for h in range(HALVES)]
-        s1 = [sb.tile([P, JH], F32, name="s1_%d" % h) for h in range(HALVES)]
-        y = [sb.tile([P, JH], F32, name="y_%d" % h) for h in range(HALVES)]
+        def halves(name):
+            return [sb.tile([P, JH], F32, name="%s_%d" % (name, h)) for h in range(HALVES)]
+
+        neg_th1, gate_term, inner, gated, y = (halves(n) for n in ("neg_th1", "gate_term", "inner", "gated", "y"))
         for h in range(HALVES):
-            nc.vector.scalar_tensor_tensor(m1[h][:], tas[h][:], og_sb[:], fa[h][:], ALU.mult, ALU.mult)
-            nc.vector.scalar_tensor_tensor(m2[h][:], tbs[h][:], og_sb[:], fb[h][:], ALU.mult, ALU.mult)
-            nc.vector.tensor_tensor(s1[h][:], base_sb[:, cols(h)], m1[h][:], ALU.subtract)
-            nc.vector.tensor_tensor(y[h][:], s1[h][:], m2[h][:], ALU.add)
+            nc.vector.scalar_tensor_tensor(neg_th1[h][:], hsqs[h][:], 1.0, tas[h][:], ALU.subtract, ALU.mult)
+            nc.vector.scalar_tensor_tensor(gate_term[h][:], tbs[h][:], 0.5, fb[h][:], ALU.mult, ALU.mult)
+            nc.vector.tensor_tensor(inner[h][:], gate_term[h][:], neg_th1[h][:], ALU.subtract)
+            nc.vector.scalar_tensor_tensor(gated[h][:], ts[h][:], 1.0, inner[h][:], ALU.add, ALU.mult)
+            nc.vector.scalar_tensor_tensor(y[h][:], gated[h][:], half_og[:], base_sb[:, cols(h)], ALU.mult, ALU.add)
             nc.sync.dma_start(out=out[:, cols(h)], in_=y[h][:])

@@ -34,7 +34,7 @@ def tile_attend_tccarrymix_kernel(
         idx = sb.tile([P, J // LIST_ROWS], U16, name="idx")
         idx2 = sb.tile([P, J // LIST_ROWS], U16, name="idx2")
         tab_w = sb.tile([P, T], I32, name="tab_w", align_bytes=64)
-        dtab_w = sb.tile([P, T], I32, name="dtab_w", align_bytes=64)
+        dtab_w = sb.tile([P, T], I32, name="dtab_w", tag="dtab_then_fa", align_bytes=64)
         tab_s = sb.tile([P, T], U8, name="tab_s", align_bytes=64)
         dtab_s = sb.tile([P, T], U8, name="dtab_s", align_bytes=64)
         w1_raw = sb.tile([P, PACK, R], F32, name="w1_raw")
@@ -57,12 +57,12 @@ def tile_attend_tccarrymix_kernel(
         nc.vector.memset(tab_s[:].bitcast(I32), 0)
         nc.vector.memset(dtab_s[:].bitcast(I32), 0)
         nc.sync.dma_start(idx[:], offs)
-        nc.sync.dma_start(idx2[:], offs2)
         nc.sync.dma_start(out=w1_raw[:], in_=w1.rearrange("(p j) r -> p j r", j=PACK))
+        nc.sync.dma_start(out=w2_raw[:], in_=w2.rearrange("(p j) r -> p j r", j=PACK))
         load_scales(tab_s, tab_scales, 0)
         load_words(tab_w, tab_words)
+        nc.sync.dma_start(idx2[:], offs2)
         load_scales(dtab_s, dtab_scales, DTAB_PLANE)
-        nc.sync.dma_start(out=w2_raw[:], in_=w2.rearrange("(p j) r -> p j r", j=PACK))
         nc.sync.dma_start(out=carry_sb[:], in_=carry)
         load_words(dtab_w, dtab_words)
         nc.sync.dma_start(out=base_sb[:], in_=base)
@@ -71,7 +71,7 @@ def tile_attend_tccarrymix_kernel(
         half_bias = sb.tile([P, 1], F32, name="half_bias")
         half_og = sb.tile([P, 1], F32, name="half_og")
         nc.gpsimd.tensor_scalar(half_bias[:], bias_sb[:], 0.5, None, ALU.mult)
-        nc.gpsimd.tensor_scalar(half_og[:], og_sb[:], 0.5, None, ALU.mult)
+        nc.gpsimd.tensor_scalar(half_og[:], og_sb[:], 0.25, None, ALU.mult)
 
         def quantise(raw, name):
             grouped = sb.tile([P, R, PACK], BF16, name=name + "_g", align_bytes=64)
@@ -90,14 +90,14 @@ def tile_attend_tccarrymix_kernel(
         def cols(h):
             return slice(h * JH, (h + 1) * JH)
 
-        def product(name, wq, words, plane, first, h):
-            acc = ps.tile([P, JH], F32, name=name)
+        def product(name, wq, words, plane, width):
+            acc = ps.tile([P, width], F32, name=name)
             nc.tensor.matmul_mx(
                 out=acc[:],
                 lhsT=wq[0][:].bitcast(FP8X4),
                 lhsT_scale=wq[1][:],
                 rhs=words[:].bitcast(FP8X4),
-                rhs_scale=plane[first:P, cols(h)],
+                rhs_scale=plane,
                 start=True,
                 stop=True,
             )
@@ -108,51 +108,40 @@ def tile_attend_tccarrymix_kernel(
         w1q = quantise(w1_raw, "w1")
         w2q = quantise(w2_raw, "w2")
 
-        hs, ts, hsqs = [], [], []
+        def full(name, tag=""):
+            return sb.tile([P, J], F32, name=name, tag=tag or name, align_bytes=64)
+
+        h1, th, hsq, tsq, diff = (full(n) for n in ("h1", "th", "hsq", "tsq", "diff"))
+        dtanh = full("dtanh", "dtanh_then_fb")
         for h in range(HALVES):
             tg = sb.tile([P, JH], U32, name="tab_g%d" % h, align_bytes=64)
             nc.vector.tensor_copy(tg[:], tab_w[:].bitcast(U32).indirect(half_list(idx, h)))
-            a = product("a%d" % h, w1q, tg, tab_sg, 0, h)
-            b = product("b%d" % h, w2q, tg, tab_sg, 0, h)
-            h1 = sb.tile([P, JH], F32, name="h1_%d" % h)
-            th = sb.tile([P, JH], F32, name="th_%d" % h)
-            hsq = sb.tile([P, JH], F32, name="hsq_%d" % h)
-            nc.scalar.activation(h1[:], a[:], ACT.Tanh)
-            nc.scalar.activation(th[:], b[:], ACT.Tanh, bias=half_bias[:], scale=0.5)
-            nc.scalar.activation(hsq[:], h1[:], ACT.Square)
-            hs.append(h1)
-            ts.append(th)
-            hsqs.append(hsq)
+            a = product("a%d" % h, w1q, tg, tab_sg[:, cols(h)], JH)
+            b = product("b%d" % h, w2q, tg, tab_sg[:, cols(h)], JH)
+            nc.scalar.activation(h1[:, cols(h)], a[:], ACT.Tanh)
+            nc.scalar.activation(th[:, cols(h)], b[:], ACT.Tanh, bias=half_bias[:], scale=0.5)
+        nc.scalar.activation(hsq[:], h1[:], ACT.Square)
+        nc.scalar.activation(dtanh[:], hsq[:], ACT.Copy, bias=2.0, scale=-2.0)
+        nc.scalar.activation(tsq[:], th[:], ACT.Square)
 
         dtab_sg = sb.tile([P, J], U8, name="dtab_sg", align_bytes=64)
         nc.vector.tensor_copy(dtab_sg[:], dtab_s[:].indirect(idx[:]))
+        nc.vector.tensor_tensor(diff[:], carry_sb[:].indirect(idx2[:]), h1[:], ALU.subtract)
+        dtab_g = sb.tile([P, J], U32, name="dtab_g", align_bytes=64)
+        nc.vector.tensor_copy(dtab_g[:], dtab_w[:].bitcast(U32).indirect(idx[:]))
+        ta = product("ta", w1q, dtab_g, dtab_sg[DTAB_PLANE:P, :], J)
+        tb = product("tb", w2q, dtab_g, dtab_sg[DTAB_PLANE:P, :], J)
 
-        diffs = []
-        for h in range(HALVES):
-            diff = sb.tile([P, JH], F32, name="diff%d" % h)
-            nc.vector.tensor_tensor(diff[:], carry_sb[:].indirect(half_list(idx2, h)), hs[h][:], ALU.subtract)
-            diffs.append(diff)
-        fb = []
-        for h in range(HALVES):
-            fac_b = sb.tile([P, JH], F32, name="fac_b%d" % h)
-            nc.vector.scalar_tensor_tensor(fac_b[:], ts[h][:], 1.0, diffs[h][:], ALU.subtract, ALU.mult)
-            fb.append(fac_b)
+        fa = full("fa", "dtab_then_fa")
+        nc.vector.scalar_tensor_tensor(fa[:], th[:], 1.0, dtanh[:], ALU.add, ALU.mult)
+        fb = full("fb", "dtanh_then_fb")
+        nc.vector.scalar_tensor_tensor(fb[:], tsq[:], 1.0, diff[:], ALU.subtract, ALU.mult)
 
-        tas, tbs = [], []
+        m1, m2, s1, y = (full(n) for n in ("m1", "m2", "s1", "y"))
+        nc.vector.scalar_tensor_tensor(m1[:], ta[:], half_og[:], fa[:], ALU.mult, ALU.mult)
+        nc.vector.scalar_tensor_tensor(m2[:], tb[:], half_og[:], fb[:], ALU.mult, ALU.mult)
         for h in range(HALVES):
-            dg = sb.tile([P, JH], U32, name="dtab_g%d" % h, align_bytes=64)
-            nc.vector.tensor_copy(dg[:], dtab_w[:].bitcast(U32).indirect(half_list(idx, h)))
-            tas.append(product("ta%d" % h, w1q, dg, dtab_sg, DTAB_PLANE, h))
-            tbs.append(product("tb%d" % h, w2q, dg, dtab_sg, DTAB_PLANE, h))
-
-        def halves(name):
-            return [sb.tile([P, JH], F32, name="%s_%d" % (name, h)) for h in range(HALVES)]
-
-        neg_th1, gate_term, inner, gated, y = (halves(n) for n in ("neg_th1", "gate_term", "inner", "gated", "y"))
+            nc.vector.tensor_tensor(s1[:, cols(h)], base_sb[:, cols(h)], m1[:, cols(h)], ALU.add)
         for h in range(HALVES):
-            nc.vector.scalar_tensor_tensor(neg_th1[h][:], hsqs[h][:], 1.0, tas[h][:], ALU.subtract, ALU.mult)
-            nc.vector.scalar_tensor_tensor(gate_term[h][:], tbs[h][:], 0.5, fb[h][:], ALU.mult, ALU.mult)
-            nc.vector.tensor_tensor(inner[h][:], gate_term[h][:], neg_th1[h][:], ALU.subtract)
-            nc.vector.scalar_tensor_tensor(gated[h][:], ts[h][:], 1.0, inner[h][:], ALU.add, ALU.mult)
-            nc.vector.scalar_tensor_tensor(y[h][:], gated[h][:], half_og[:], base_sb[:, cols(h)], ALU.mult, ALU.add)
-            nc.sync.dma_start(out=out[:, cols(h)], in_=y[h][:])
+            nc.vector.tensor_tensor(y[:, cols(h)], s1[:, cols(h)], m2[:, cols(h)], ALU.add)
+            nc.sync.dma_start(out=out[:, cols(h)], in_=y[:, cols(h)])

@@ -34,7 +34,7 @@ def tile_attend_tccarrymix_kernel(
         idx = sb.tile([P, J // LIST_ROWS], U16, name="idx")
         idx2 = sb.tile([P, J // LIST_ROWS], U16, name="idx2")
         tab_w = sb.tile([P, T], I32, name="tab_w", align_bytes=64)
-        dtab_w = sb.tile([P, T], I32, name="dtab_w", tag="dtab_then_fa", align_bytes=64)
+        dtab_w = sb.tile([P, T], I32, name="dtab_w", tag="dtab_then_fb", align_bytes=64)
         tab_s = sb.tile([P, T], U8, name="tab_s", align_bytes=64)
         dtab_s = sb.tile([P, T], U8, name="dtab_s", align_bytes=64)
         w1_raw = sb.tile([P, PACK, R], F32, name="w1_raw")
@@ -111,8 +111,8 @@ def tile_attend_tccarrymix_kernel(
         def full(name, tag=""):
             return sb.tile([P, J], F32, name=name, tag=tag or name, align_bytes=64)
 
-        h1, th, hsq, tsq, diff = (full(n) for n in ("h1", "th", "hsq", "tsq", "diff"))
-        dtanh = full("dtanh", "dtanh_then_fb")
+        th, hsq, dtanh, gate, tsq, diff = (full(n) for n in ("th", "hsq", "dtanh", "gate", "tsq", "diff"))
+        h1 = full("h1", "h1_then_fa")
         for h in range(HALVES):
             tg = sb.tile([P, JH], U32, name="tab_g%d" % h, align_bytes=64)
             nc.vector.tensor_copy(tg[:], tab_w[:].bitcast(U32).indirect(half_list(idx, h)))
@@ -122,6 +122,7 @@ def tile_attend_tccarrymix_kernel(
             nc.scalar.activation(th[:, cols(h)], b[:], ACT.Tanh, bias=half_bias[:], scale=0.5)
         nc.scalar.activation(hsq[:], h1[:], ACT.Square)
         nc.scalar.activation(dtanh[:], hsq[:], ACT.Copy, bias=2.0, scale=-2.0)
+        nc.scalar.activation(gate[:], th[:], ACT.Copy, bias=1.0)
         nc.scalar.activation(tsq[:], th[:], ACT.Square)
 
         dtab_sg = sb.tile([P, J], U8, name="dtab_sg", align_bytes=64)
@@ -132,13 +133,14 @@ def tile_attend_tccarrymix_kernel(
         ta = product("ta", w1q, dtab_g, dtab_sg[DTAB_PLANE:P, :], J)
         tb = product("tb", w2q, dtab_g, dtab_sg[DTAB_PLANE:P, :], J)
 
-        fa = full("fa", "dtab_then_fa")
-        nc.vector.scalar_tensor_tensor(fa[:], th[:], 1.0, dtanh[:], ALU.add, ALU.mult)
-        fb = full("fb", "dtanh_then_fb")
+        fa = full("fa", "h1_then_fa")
+        nc.gpsimd.tensor_tensor(fa[:], dtanh[:], gate[:], ALU.mult)
+        fb = full("fb", "dtab_then_fb")
         nc.vector.scalar_tensor_tensor(fb[:], tsq[:], 1.0, diff[:], ALU.subtract, ALU.mult)
 
-        m1, m2, s1, y = (full(n) for n in ("m1", "m2", "s1", "y"))
+        m1, s1, y = (full(n) for n in ("m1", "s1", "y"))
         nc.vector.scalar_tensor_tensor(m1[:], ta[:], half_og[:], fa[:], ALU.mult, ALU.mult)
+        m2 = full("m2", "h1_then_fa")
         nc.vector.scalar_tensor_tensor(m2[:], tb[:], half_og[:], fb[:], ALU.mult, ALU.mult)
         for h in range(HALVES):
             nc.vector.tensor_tensor(s1[:, cols(h)], base_sb[:, cols(h)], m1[:, cols(h)], ALU.add)

from contextlib import ExitStack

import concourse.mybir as mybir

K, R, T, J, U = 512, 128, 2048, 512, 1024
FLOPS = 4 * 2 * K * R * J

F32 = mybir.dt.float32
BF16 = mybir.dt.bfloat16
I32 = mybir.dt.int32
U32 = mybir.dt.uint32
U16 = mybir.dt.uint16
U8 = mybir.dt.uint8
FP8X4 = mybir.dt.float8_e4m3fn_x4
ACT = mybir.ActivationFunctionType
ALU = mybir.AluOpType

P = 128
PACK = 4
HALVES = 2
JH = J // HALVES
LIST_ROWS = 16
DTAB_PLANE = 4


def tile_attend_tccarrymix_kernel(
    tc, tab_words, tab_scales, dtab_words, dtab_scales, w1, w2, bias, carry, og, base, offs, offs2, out
):
    nc = tc.nc
    with ExitStack() as ctx:
        sb = ctx.enter_context(tc.tile_pool(name="sb", bufs=1))
        ps = ctx.enter_context(tc.psum_pool(name="ps", bufs=1))

        idx = sb.tile([P, J // LIST_ROWS], U16, name="idx")
        idx2 = sb.tile([P, J // LIST_ROWS], U16, name="idx2")
        tab_w = sb.tile([P, T], I32, name="tab_w", align_bytes=64)
        dtab_w = sb.tile([P, T], I32, name="dtab_w", tag="dtab_then_fb", align_bytes=64)
        tab_s = sb.tile([P, T], U8, name="tab_s", align_bytes=64)
        dtab_s = sb.tile([P, T], U8, name="dtab_s", align_bytes=64)
        w1_raw = sb.tile([P, PACK, R], F32, name="w1_raw")
        w2_raw = sb.tile([P, PACK, R], F32, name="w2_raw")
        carry_sb = sb.tile([P, U], F32, name="carry_sb")
        base_sb = sb.tile([P, J], F32, name="base_sb")
        bias_sb = sb.tile([P, 1], F32, name="bias_sb")
        og_sb = sb.tile([P, 1], F32, name="og_sb")

        def load_scales(plane, src, first):
            rows = src[0].bitcast(I32)
            for q in range(4):
                nc.sync.dma_start(
                    out=plane[32 * q + first : 32 * q + first + 4, :].bitcast(I32), in_=rows[4 * q : 4 * q + 4, :]
                )

        def load_words(dst, src):
            nc.sync.dma_start(out=dst[:], in_=src[0].rearrange("p n t -> p (n t)").bitcast(I32))

        nc.vector.memset(tab_s[:].bitcast(I32), 0)
        nc.vector.memset(dtab_s[:].bitcast(I32), 0)
        nc.sync.dma_start(idx[:], offs)
        nc.sync.dma_start(out=w1_raw[:], in_=w1.rearrange("(p j) r -> p j r", j=PACK))
        nc.sync.dma_start(out=w2_raw[:], in_=w2.rearrange("(p j) r -> p j r", j=PACK))
        load_scales(tab_s, tab_scales, 0)
        load_words(tab_w, tab_words)
        nc.sync.dma_start(idx2[:], offs2)
        load_scales(dtab_s, dtab_scales, DTAB_PLANE)
        nc.sync.dma_start(out=carry_sb[:], in_=carry)
        load_words(dtab_w, dtab_words)
        nc.sync.dma_start(out=base_sb[:], in_=base)
        nc.gpsimd.dma_start(out=bias_sb[:], in_=bias)
        nc.gpsimd.dma_start(out=og_sb[:], in_=og)
        half_bias = sb.tile([P, 1], F32, name="half_bias")
        half_og = sb.tile([P, 1], F32, name="half_og")
        nc.gpsimd.tensor_scalar(half_bias[:], bias_sb[:], 0.5, None, ALU.mult)
        nc.gpsimd.tensor_scalar(half_og[:], og_sb[:], 0.25, None, ALU.mult)

        def quantise(raw, name):
            grouped = sb.tile([P, R, PACK], BF16, name=name + "_g", align_bytes=64)
            nc.scalar.copy(out=grouped[:], in_=raw[:].rearrange("p j r -> p r j"))
            codes = sb.tile([P, R], U32, name=name + "_c", align_bytes=64)
            scales = sb.tile([P, R], U8, name=name + "_s", align_bytes=64)
            nc.vector.quantize_mx(
                out=codes[:].bitcast(FP8X4), scales=scales[:], in_=grouped[:].rearrange("p r j -> p (r j)")
            )
            return codes, scales

        def half_list(lst, h):
            n = JH // LIST_ROWS
            return lst[:, h * n : (h + 1) * n]

        def cols(h):
            return slice(h * JH, (h + 1) * JH)

        def product(name, wq, words, plane, width):
            acc = ps.tile([P, width], F32, name=name)
            nc.tensor.matmul_mx(
                out=acc[:],
                lhsT=wq[0][:].bitcast(FP8X4),
                lhsT_scale=wq[1][:],
                rhs=words[:].bitcast(FP8X4),
                rhs_scale=plane,
                start=True,
                stop=True,
            )
            return acc

        tab_sg = sb.tile([P, J], U8, name="tab_sg", align_bytes=64)
        nc.vector.tensor_copy(tab_sg[:], tab_s[:].indirect(idx[:]))
        w1q = quantise(w1_raw, "w1")
        w2q = quantise(w2_raw, "w2")

        def full(name, tag=""):
            return sb.tile([P, J], F32, name=name, tag=tag or name, align_bytes=64)

        th, hsq, dtanh, gate, tsq, diff = (full(n) for n in ("th", "hsq", "dtanh", "gate", "tsq", "diff"))
        h1 = full("h1", "h1_then_fa")
        for h in range(HALVES):
            tg = sb.tile([P, JH], U32, name="tab_g%d" % h, align_bytes=64)
            nc.vector.tensor_copy(tg[:], tab_w[:].bitcast(U32).indirect(half_list(idx, h)))
            a = product("a%d" % h, w1q, tg, tab_sg[:, cols(h)], JH)
            b = product("b%d" % h, w2q, tg, tab_sg[:, cols(h)], JH)
            nc.scalar.activation(h1[:, cols(h)], a[:], ACT.Tanh)
            nc.scalar.activation(th[:, cols(h)], b[:], ACT.Tanh, bias=half_bias[:], scale=0.5)
        nc.scalar.activation(hsq[:], h1[:], ACT.Square)
        nc.scalar.activation(dtanh[:], hsq[:], ACT.Copy, bias=2.0, scale=-2.0)
        nc.scalar.activation(gate[:], th[:], ACT.Copy, bias=1.0)
        nc.scalar.activation(tsq[:], th[:], ACT.Square)

        dtab_sg = sb.tile([P, J], U8, name="dtab_sg", align_bytes=64)
        nc.vector.tensor_copy(dtab_sg[:], dtab_s[:].indirect(idx[:]))
        nc.vector.tensor_tensor(diff[:], carry_sb[:].indirect(idx2[:]), h1[:], ALU.subtract)
        dtab_g = sb.tile([P, J], U32, name="dtab_g", align_bytes=64)
        nc.vector.tensor_copy(dtab_g[:], dtab_w[:].bitcast(U32).indirect(idx[:]))
        ta = product("ta", w1q, dtab_g, dtab_sg[DTAB_PLANE:P, :], J)
        tb = product("tb", w2q, dtab_g, dtab_sg[DTAB_PLANE:P, :], J)

        fa = full("fa", "h1_then_fa")
        nc.gpsimd.tensor_tensor(fa[:], dtanh[:], gate[:], ALU.mult)
        fb = full("fb", "dtab_then_fb")
        nc.vector.scalar_tensor_tensor(fb[:], tsq[:], 1.0, diff[:], ALU.subtract, ALU.mult)

        m1, s1, y = (full(n) for n in ("m1", "s1", "y"))
        nc.vector.scalar_tensor_tensor(m1[:], ta[:], half_og[:], fa[:], ALU.mult, ALU.mult)
        m2 = full("m2", "h1_then_fa")
        nc.vector.scalar_tensor_tensor(m2[:], tb[:], half_og[:], fb[:], ALU.mult, ALU.mult)
        for h in range(HALVES):
            nc.vector.tensor_tensor(s1[:, cols(h)], base_sb[:, cols(h)], m1[:, cols(h)], ALU.add)
        for h in range(HALVES):
            nc.vector.tensor_tensor(y[:, cols(h)], s1[:, cols(h)], m2[:, cols(h)], ALU.add)
            nc.sync.dma_start(out=out[:, cols(h)], in_=y[:, cols(h)])
